import numpy as np
import ml_dtypes


def mxq(x, axis, fmt="e4m3"):
    dtype, down = {"e4m3": (ml_dtypes.float8_e4m3fn, 7), "e5m2": (ml_dtypes.float8_e5m2, 14)}[fmt]
    v = np.moveaxis(np.asarray(x, np.float32).astype(ml_dtypes.bfloat16).astype(np.float64), axis, -1)
    blocks = v.reshape(v.shape[:-1] + (-1, 32))
    amax = np.abs(blocks).max(-1, keepdims=True)
    byte = np.maximum(np.where(amax > 0, np.frexp(amax)[1] - 1 + 127, 0) - down, 1)
    scale = np.exp2(byte - 127.0)
    codes = (blocks / scale).astype(np.float32).astype(dtype).astype(np.float64)
    return np.moveaxis((codes * scale).reshape(v.shape), -1, axis)


WIDE = False


def mx_kscale(k):
    if not WIDE:
        return np.ones(k)
    levels = np.array([24, -24, 12, -12, 0])
    if k % 512:
        return np.exp2(np.random.permutation(np.resize(levels, k // 32))).repeat(32)
    a = np.empty((k // 512, 16))
    for p in range(k // 512):
        a[p, :8] = np.random.permutation(np.resize(levels, 8))
        for g in range(8):
            far = levels[np.abs(levels - a[p, g]) >= 10]
            a[p, g + 8] = far[np.random.randint(len(far))]
    return np.exp2(a.ravel()).repeat(32)


def f64(x):
    return np.asarray(x).astype(np.float64)


def striped8(idx):
    return np.concatenate([v.reshape(-1, 16).T for v in idx]).astype(np.uint16)


def unstriped8(offs):
    return np.stack([offs[16 * g:16 * g + 16].T.reshape(-1) for g in range(8)]).astype(np.int64)


E2M1 = np.array([0.0, 0.5, 1.0, 1.5, 2.0, 3.0, 4.0, 6.0, -0.0, -0.5, -1.0, -1.5, -2.0, -3.0, -4.0, -6.0])


def pack_weight(w, fmt):
    k, n = w.shape
    w = f64(np.asarray(w, np.float32).astype(ml_dtypes.bfloat16)).reshape(k // 32, 32, n)
    amax = np.abs(w).max(1)
    if fmt == "e4m3":
        byte = np.frexp(amax)[1] - 1 + 127 - 7
    else:
        mant, ex = np.frexp(amax / 6.0)
        byte = np.where(mant > 0.5, ex, ex - 1) + 127
    byte = np.clip(np.where(amax > 0, byte, 1), 1, 254)
    scaled = (w * np.exp2(127.0 - byte)[:, None, :]).reshape(k, n).astype(np.float32)
    by_word = np.ascontiguousarray(scaled.reshape(k // 512, 128, 4, n).transpose(0, 1, 3, 2))
    if fmt == "e4m3":
        words = by_word.astype(ml_dtypes.float8_e4m3fn).view(np.uint8)
    else:
        c = by_word.astype(ml_dtypes.float4_e2m1fn).view(np.uint8) & 0xF
        words = (c[..., 0::2] | (c[..., 1::2] << 4)).reshape(k // 512, 128, 2 * n)
    return np.ascontiguousarray(words), np.ascontiguousarray(byte.astype(np.uint8).reshape(k // 512, 16, n))


def unpack_weight(words, scales, fmt):
    g, _, n = scales.shape
    words = np.ascontiguousarray(words).reshape(g, 128, n, -1)
    if fmt == "e4m3":
        vals = words.view(ml_dtypes.float8_e4m3fn).astype(np.float64)
    else:
        nib = np.empty((g, 128, n, 4), np.uint8)
        nib[..., 0::2] = words & 0xF
        nib[..., 1::2] = words >> 4
        vals = E2M1[nib]
    vals = vals * np.repeat(np.exp2(scales.astype(np.float64) - 127.0), 8, axis=1)[..., None]
    return vals.transpose(0, 1, 3, 2).reshape(g * 512, n)


def planes(y):
    n, m = y.shape
    v = y.astype(np.float32).astype(ml_dtypes.bfloat16).astype(np.float64).reshape(n // 32, 32, m)
    top = np.abs(v).max(1)
    byte = np.clip(np.where(top > 0, np.frexp(top)[1] - 1 + 127 - 7, 1), 1, 254)
    codes = (v * np.exp2(127.0 - byte)[:, None, :]).reshape(n, m).astype(np.float32).astype(ml_dtypes.float8_e4m3fn).view(np.uint8)
    words = codes.reshape(n // 512, 128, 4, m).transpose(0, 1, 3, 2)
    return np.ascontiguousarray(words), np.ascontiguousarray(byte.astype(np.uint8).reshape(n // 512, 16, m))


def silu(f):
    return f / (1.0 + np.exp(-np.maximum(f, -700.0)))


K, L, N, T, J = 512, 512, 512, 2048, 1024


def setup_inputs():
    n = np.random.standard_normal
    s = mx_kscale(K)[:, None]
    s2 = mx_kscale(L)[:, None]
    p_wa = pack_weight(n((K, N)) / np.sqrt(K) / s, "e4m3")
    p_wb = pack_weight(n((L, N)) / np.sqrt(L) / s2, "e4m3")
    return {
        "xT": (n((K, T)) * s).astype(np.float32),
        "wgt": np.repeat(np.random.uniform(0.5, 2.0, (8, J)), 16, axis=0).astype(np.float32),
        "zT": (n((L, T)) * s2).astype(np.float32),
        "wgt2": np.repeat(np.random.uniform(0.5, 2.0, (8, J)), 16, axis=0).astype(np.float32),
        "wa_words": p_wa[0],
        "wa_scales": p_wa[1],
        "wb_words": p_wb[0],
        "wb_scales": p_wb[1],
        "res": (n((N, J))).astype(np.float32),
        "offs": striped8(np.stack([np.random.permutation(T)[:J] for _ in range(8)])),
        "offs2": striped8(np.stack([np.random.permutation(T)[:J] for _ in range(8)])),
    }


def reference(xT, wgt, zT, wgt2, wa_words, wa_scales, wb_words, wb_scales, res, offs, offs2):
    idx = unstriped8(offs)
    idx2 = unstriped8(offs2)
    rows = np.arange(K)
    xg = f64(wgt)[rows // 4 % 128] * f64(xT)[rows[:, None], idx[rows % 512 // 64]]
    xT_ = mxq(xg, 0, "e4m3")
    rows = np.arange(L)
    xg = f64(wgt2)[rows // 4 % 128] * f64(zT)[rows[:, None], idx2[rows % 512 // 64]]
    zT_ = mxq(xg, 0, "e4m3")
    wa_ = unpack_weight(wa_words, wa_scales, "e4m3")
    wb_ = unpack_weight(wb_words, wb_scales, "e4m3")
    ya = wa_.T @ xT_
    yb = wb_.T @ zT_
    out_0 = silu(ya) * yb + f64(res)
    return (out_0,) + planes(out_0)

@@ -1,0 +1,164 @@
+from contextlib import ExitStack
+
+import concourse.mybir as mybir
+from concourse.masks import make_identity
+
+K, N, T, J = 512, 512, 2048, 1024
+FLOPS = 2 * 2 * K * N * J
+
+F32 = mybir.dt.float32
+BF16 = mybir.dt.bfloat16
+I32 = mybir.dt.int32
+U32 = mybir.dt.uint32
+U16 = mybir.dt.uint16
+U8 = mybir.dt.uint8
+FP8X4 = mybir.dt.float8_e4m3fn_x4
+MULT = mybir.AluOpType.mult
+ADD = mybir.AluOpType.add
+SILU = mybir.ActivationFunctionType.Silu
+
+P = 128
+PACK = 4
+BLK = 128
+X_CHUNK = 512
+Z_CHUNK = 256
+OUT_CHUNK = 256
+
+
+def tile_list_glu_resP_kernel(
+    tc, xT, wgt, zT, wgt2, wa_words, wa_scales, wb_words, wb_scales, res, offs, offs2, out_0, out_1, out_2
+):
+    nc = tc.nc
+    with ExitStack() as ctx:
+        keep = ctx.enter_context(tc.tile_pool(name="keep", bufs=1))
+        ring = ctx.enter_context(tc.tile_pool(name="ring", bufs=3))
+        ps_a = ctx.enter_context(tc.psum_pool(name="ps_a", bufs=2))
+        ps_b = ctx.enter_context(tc.psum_pool(name="ps_b", bufs=3))
+        ps_o = ctx.enter_context(tc.psum_pool(name="ps_o", bufs=3))
+
+        x_list = keep.tile([P, J // 16], U16, name="x_list")
+        z_list = keep.tile([P, J // 16], U16, name="z_list")
+        x_planes = [keep.tile([P, T], F32, name=f"x_plane{i}") for i in range(PACK)]
+        z_planes = [keep.tile([P, T], F32, name=f"z_plane{i}") for i in range(PACK)]
+        x_wgt = [keep.tile([P, X_CHUNK], F32, name=f"x_wgt{c}") for c in range(J // X_CHUNK)]
+        z_wgt = keep.tile([P, J], F32, name="z_wgt")
+        wa_codes = keep.tile([P, N], U32, name="wa_codes", align_bytes=64)
+        wb_codes = keep.tile([P, N], U32, name="wb_codes", align_bytes=64)
+        wa_plane = keep.tile([P, N], U8, name="wa_plane", align_bytes=64)
+        wb_plane = keep.tile([P, N], U8, name="wb_plane", align_bytes=64)
+        res_t = [keep.tile([P, PACK, OUT_CHUNK], F32, name=f"res{c}") for c in range(J // OUT_CHUNK)]
+        ident = keep.tile([P, P], F32, name="ident")
+
+        x_rows = xT.rearrange("(p i) t -> p i t", i=PACK)
+        z_rows = zT.rearrange("(p i) t -> p i t", i=PACK)
+        res_rows = res.rearrange("(p i) j -> p i j", i=PACK)
+        out_rows = out_0.rearrange("(p i) j -> p i j", i=PACK)
+        out_words = out_1[0].rearrange("p j i -> p (j i)").bitcast(I32)
+
+        for plane, scales in ((wa_plane, wa_scales), (wb_plane, wb_scales)):
+            nc.gpsimd.memset(plane[:].bitcast(U32), 0)
+        make_identity(nc, ident[:])
+        for plane, scales in ((wa_plane, wa_scales), (wb_plane, wb_scales)):
+            for q in range(4):
+                nc.gpsimd.dma_start(
+                    out=plane[32 * q : 32 * q + 4, :].bitcast(I32),
+                    in_=scales[0, 4 * q : 4 * q + 4, :].bitcast(I32),
+                )
+
+        nc.sync.dma_start(x_list[:], offs)
+        nc.sync.dma_start(out=x_planes[0][:], in_=x_rows[:, 0, :])
+        for c in range(J // X_CHUNK):
+            nc.sync.dma_start(out=x_wgt[c][:], in_=wgt[:, c * X_CHUNK : (c + 1) * X_CHUNK])
+        for i in range(1, PACK):
+            nc.sync.dma_start(out=x_planes[i][:], in_=x_rows[:, i, :])
+        nc.sync.dma_start(z_list[:], offs2)
+        nc.sync.dma_start(out=wa_codes[:].bitcast(I32), in_=wa_words[0].rearrange("p n i -> p (n i)").bitcast(I32))
+        nc.sync.dma_start(out=z_wgt[:], in_=wgt2)
+        for i in range(PACK):
+            nc.sync.dma_start(out=z_planes[i][:], in_=z_rows[:, i, :])
+        nc.sync.dma_start(out=wb_codes[:].bitcast(I32), in_=wb_words[0].rearrange("p n i -> p (n i)").bitcast(I32))
+        for c in range(J // OUT_CHUNK):
+            nc.sync.dma_start(out=res_t[c][:], in_=res_rows[:, :, c * OUT_CHUNK : (c + 1) * OUT_CHUNK])
+
+        def gather(picked, planes, offsets, weights, i, j0, width):
+            cols = offsets[:, j0 // 16 : (j0 + width) // 16]
+            nc.vector.tensor_tensor(picked[:, i, :], planes[i][:].indirect(cols), weights, MULT)
+
+        def round_and_interleave(source, name):
+            width = source.shape[2]
+            grouped = keep.tile([P, width * PACK], BF16, name=name, align_bytes=64)
+            nc.scalar.copy(
+                out=grouped[:].rearrange("p (c m i) -> p c i m", m=4, i=PACK),
+                in_=source[:].rearrange("p i (c m) -> p c i m", m=4),
+            )
+            return grouped
+
+        def quantize(grouped, name):
+            width = grouped.shape[1] // PACK
+            codes = keep.tile([P, width], U32, name=name + "_codes", align_bytes=64)
+            plane = keep.tile([P, width], U8, name=name + "_plane", align_bytes=64)
+            nc.vector.quantize_mx(out=codes[:].bitcast(FP8X4), scales=plane[:], in_=grouped[:])
+            return codes, plane
+
+        def product(bank, codes, plane, c0, w_codes, w_plane):
+            nc.tensor.matmul_mx(
+                out=bank[:],
+                lhsT=codes[:, c0 : c0 + BLK].bitcast(FP8X4),
+                lhsT_scale=plane[:, c0 : c0 + BLK],
+                rhs=w_codes[:].bitcast(FP8X4),
+                rhs_scale=w_plane[:],
+                start=True,
+                stop=True,
+            )
+
+        x_picked = [keep.tile([P, PACK, X_CHUNK], F32, name=f"x_picked{c}") for c in range(J // X_CHUNK)]
+        for i in range(2):
+            for c in range(J // X_CHUNK):
+                gather(x_picked[c], x_planes, x_list, x_wgt[c][:], i, c * X_CHUNK, X_CHUNK)
+        gates = []
+        for c in range(J // X_CHUNK):
+            for i in range(2, PACK):
+                gather(x_picked[c], x_planes, x_list, x_wgt[c][:], i, c * X_CHUNK, X_CHUNK)
+            codes, plane = quantize(round_and_interleave(x_picked[c], f"x_bf{c}"), f"xq{c}")
+            for c0 in range(0, X_CHUNK, BLK):
+                bank = ps_a.tile([P, N], F32, name="ya")
+                product(bank, codes, plane, c0, wa_codes, wa_plane)
+                gate = keep.tile([P, PACK, P], F32, name=f"gate{len(gates)}")
+                nc.scalar.activation(out=gate[:], in_=bank[:].rearrange("j (q i) -> j i q", i=PACK), func=SILU)
+                gates.append(gate)
+
+        z_picked = [keep.tile([P, PACK, Z_CHUNK], F32, name=f"z_picked{c}") for c in range(J // Z_CHUNK)]
+        for i in range(PACK - 1):
+            for c in range(J // Z_CHUNK):
+                j0 = c * Z_CHUNK
+                gather(z_picked[c], z_planes, z_list, z_wgt[:, j0 : j0 + Z_CHUNK], i, j0, Z_CHUNK)
+        out_plane = keep.tile([P, J], U8, name="out_plane", align_bytes=64)
+        for c in range(J // Z_CHUNK):
+            j0 = c * Z_CHUNK
+            gather(z_picked[c], z_planes, z_list, z_wgt[:, j0 : j0 + Z_CHUNK], PACK - 1, j0, Z_CHUNK)
+            codes, plane = quantize(round_and_interleave(z_picked[c], f"z_bf{c}"), f"zq{c}")
+            result = keep.tile([P, PACK, OUT_CHUNK], F32, name=f"result{c}")
+            for c0 in range(0, Z_CHUNK, BLK):
+                bank = ps_b.tile([P, N], F32, name="yb")
+                product(bank, codes, plane, c0, wb_codes, wb_plane)
+                gated = ring.tile([P, PACK, P], F32, name="gated")
+                nc.vector.tensor_tensor(
+                    gated[:], bank[:].rearrange("j (q i) -> j i q", i=PACK), gates[(j0 + c0) // BLK][:], MULT
+                )
+                turned = ps_o.tile([P, PACK, BLK], F32, name="turned")
+                for i in range(PACK):
+                    nc.tensor.transpose(turned[:, i, :], gated[:, i, :], ident[:])
+                nc.vector.tensor_tensor(result[:, :, c0 : c0 + BLK], turned[:], res_t[c][:, :, c0 : c0 + BLK], ADD)
+            nc.sync.dma_start(out=out_rows[:, :, j0 : j0 + OUT_CHUNK], in_=result[:])
+            grouped = round_and_interleave(result, f"o_bf{c}")
+            o_codes = keep.tile([P, OUT_CHUNK], U32, name=f"o_codes{c}", align_bytes=64)
+            nc.vector.quantize_mx(
+                out=o_codes[:].bitcast(FP8X4), scales=out_plane[:, j0 : j0 + OUT_CHUNK], in_=grouped[:]
+            )
+            nc.sync.dma_start(out=out_words[:, j0 : j0 + OUT_CHUNK], in_=o_codes[:].bitcast(I32))
+        for q in range(4):
+            queue = nc.sync if q % 2 == 0 else nc.scalar
+            queue.dma_start(
+                out=out_2[0, 4 * q : 4 * q + 4, :].bitcast(I32),
+                in_=out_plane[32 * q : 32 * q + 4, :].bitcast(I32),
+            )

@@ -1,7 +1,6 @@
 from contextlib import ExitStack
 
 import concourse.mybir as mybir
-from concourse.masks import make_identity
 
 K, N, T, J = 512, 512, 2048, 1024
 FLOPS = 2 * 2 * K * N * J
@@ -19,10 +18,15 @@ SILU = mybir.ActivationFunctionType.Silu
 
 P = 128
 PACK = 4
-BLK = 128
-X_CHUNK = 512
-Z_CHUNK = 256
-OUT_CHUNK = 256
+BANK = 512
+WA_ROW, WB_ROW = 0, 4
+X_CHUNKS = (256, 256, 256, 256)
+Z_CHUNKS = (256, 256, 256, 128, 128)
+HALF = J // 2
+
+
+def spans(widths):
+    return [(sum(widths[:c]), w) for c, w in enumerate(widths)]
 
 
 def tile_list_glu_resP_kernel(
@@ -31,23 +35,22 @@ def tile_list_glu_resP_kernel(
     nc = tc.nc
     with ExitStack() as ctx:
         keep = ctx.enter_context(tc.tile_pool(name="keep", bufs=1))
-        ring = ctx.enter_context(tc.tile_pool(name="ring", bufs=3))
-        ps_a = ctx.enter_context(tc.psum_pool(name="ps_a", bufs=2))
-        ps_b = ctx.enter_context(tc.psum_pool(name="ps_b", bufs=3))
-        ps_o = ctx.enter_context(tc.psum_pool(name="ps_o", bufs=3))
+        ps_a = ctx.enter_context(tc.psum_pool(name="ps_a", bufs=4))
+        ps_b = ctx.enter_context(tc.psum_pool(name="ps_b", bufs=4))
 
         x_list = keep.tile([P, J // 16], U16, name="x_list")
         z_list = keep.tile([P, J // 16], U16, name="z_list")
         x_planes = [keep.tile([P, T], F32, name=f"x_plane{i}") for i in range(PACK)]
         z_planes = [keep.tile([P, T], F32, name=f"z_plane{i}") for i in range(PACK)]
-        x_wgt = [keep.tile([P, X_CHUNK], F32, name=f"x_wgt{c}") for c in range(J // X_CHUNK)]
+        x_wgt = keep.tile([P, J], F32, name="x_wgt")
         z_wgt = keep.tile([P, J], F32, name="z_wgt")
         wa_codes = keep.tile([P, N], U32, name="wa_codes", align_bytes=64)
         wb_codes = keep.tile([P, N], U32, name="wb_codes", align_bytes=64)
-        wa_plane = keep.tile([P, N], U8, name="wa_plane", align_bytes=64)
-        wb_plane = keep.tile([P, N], U8, name="wb_plane", align_bytes=64)
-        res_t = [keep.tile([P, PACK, OUT_CHUNK], F32, name=f"res{c}") for c in range(J // OUT_CHUNK)]
-        ident = keep.tile([P, P], F32, name="ident")
+        wa_raw = keep.tile([P, N], U32, name="wa_raw")
+        wb_raw = keep.tile([P, N], U32, name="wb_raw")
+        w_planes_raw = keep.tile([P, N], U8, name="w_planes_raw")
+        w_planes = keep.tile([P, N], U8, name="w_planes", align_bytes=64)
+        res_t = [keep.tile([P, PACK, w], F32, name=f"res{j0}") for j0, w in spans(Z_CHUNKS)]
 
         x_rows = xT.rearrange("(p i) t -> p i t", i=PACK)
         z_rows = zT.rearrange("(p i) t -> p i t", i=PACK)
@@ -55,41 +58,58 @@ def tile_list_glu_resP_kernel(
         out_rows = out_0.rearrange("(p i) j -> p i j", i=PACK)
         out_words = out_1[0].rearrange("p j i -> p (j i)").bitcast(I32)
 
-        for plane, scales in ((wa_plane, wa_scales), (wb_plane, wb_scales)):
-            nc.gpsimd.memset(plane[:].bitcast(U32), 0)
-        make_identity(nc, ident[:])
-        for plane, scales in ((wa_plane, wa_scales), (wb_plane, wb_scales)):
-            for q in range(4):
-                nc.gpsimd.dma_start(
-                    out=plane[32 * q : 32 * q + 4, :].bitcast(I32),
-                    in_=scales[0, 4 * q : 4 * q + 4, :].bitcast(I32),
-                )
+        nc.vector.memset(w_planes_raw[:].bitcast(U32), 0)
 
-        nc.sync.dma_start(x_list[:], offs)
+        def load_scale_rows(first, scales, q):
+            nc.sync.dma_start(
+                out=w_planes_raw[32 * q + first : 32 * q + first + 4, :].bitcast(I32),
+                in_=scales[0, 4 * q : 4 * q + 4, :].bitcast(I32),
+            )
+
+        def load_words(codes, words):
+            nc.sync.dma_start(out=codes[:].bitcast(I32), in_=words[0].rearrange("p n i -> p (n i)").bitcast(I32))
+
         nc.sync.dma_start(out=x_planes[0][:], in_=x_rows[:, 0, :])
-        for c in range(J // X_CHUNK):
-            nc.sync.dma_start(out=x_wgt[c][:], in_=wgt[:, c * X_CHUNK : (c + 1) * X_CHUNK])
-        for i in range(1, PACK):
+        nc.sync.dma_start(x_list[:], offs)
+        nc.sync.dma_start(out=x_wgt[:, :HALF], in_=wgt[:, :HALF])
+        nc.sync.dma_start(out=x_wgt[:, HALF:], in_=wgt[:, HALF:])
+        for i in range(1, PACK - 1):
             nc.sync.dma_start(out=x_planes[i][:], in_=x_rows[:, i, :])
+        load_words(wa_raw, wa_words)
+        nc.sync.dma_start(out=x_planes[PACK - 1][:], in_=x_rows[:, PACK - 1, :])
+        for q in range(4):
+            load_scale_rows(WA_ROW, wa_scales, q)
         nc.sync.dma_start(z_list[:], offs2)
-        nc.sync.dma_start(out=wa_codes[:].bitcast(I32), in_=wa_words[0].rearrange("p n i -> p (n i)").bitcast(I32))
-        nc.sync.dma_start(out=z_wgt[:], in_=wgt2)
-        for i in range(PACK):
+        nc.sync.dma_start(out=z_wgt[:, :HALF], in_=wgt2[:, :HALF])
+        nc.sync.dma_start(out=z_planes[0][:], in_=z_rows[:, 0, :])
+        for q in range(4):
+            load_scale_rows(WB_ROW, wb_scales, q)
+        nc.sync.dma_start(out=z_wgt[:, HALF:], in_=wgt2[:, HALF:])
+        nc.sync.dma_start(out=z_planes[1][:], in_=z_rows[:, 1, :])
+        load_words(wb_raw, wb_words)
+        for i in range(2, PACK):
             nc.sync.dma_start(out=z_planes[i][:], in_=z_rows[:, i, :])
-        nc.sync.dma_start(out=wb_codes[:].bitcast(I32), in_=wb_words[0].rearrange("p n i -> p (n i)").bitcast(I32))
-        for c in range(J // OUT_CHUNK):
-            nc.sync.dma_start(out=res_t[c][:], in_=res_rows[:, :, c * OUT_CHUNK : (c + 1) * OUT_CHUNK])
+        for c, (j0, w) in enumerate(spans(Z_CHUNKS)):
+            nc.sync.dma_start(out=res_t[c][:], in_=res_rows[:, :, j0 : j0 + w])
+
+        def deal_columns(dealt, raw, copy):
+            copy(out=dealt[:].rearrange("p (i m) -> p i m", i=PACK), in_=raw[:].rearrange("p (m i) -> p i m", i=PACK))
+
+        deal_columns(wa_codes, wa_raw, nc.scalar.copy)
+        deal_columns(w_planes, w_planes_raw, nc.vector.tensor_copy)
+        deal_columns(wb_codes, wb_raw, nc.scalar.copy)
 
         def gather(picked, planes, offsets, weights, i, j0, width):
             cols = offsets[:, j0 // 16 : (j0 + width) // 16]
-            nc.vector.tensor_tensor(picked[:, i, :], planes[i][:].indirect(cols), weights, MULT)
+            span = slice(j0, j0 + width)
+            nc.vector.tensor_tensor(picked[:, i, span], planes[i][:].indirect(cols), weights[:, span], MULT)
 
-        def round_and_interleave(source, name):
+        def round_and_interleave(source, name, copy):
             width = source.shape[2]
             grouped = keep.tile([P, width * PACK], BF16, name=name, align_bytes=64)
-            nc.scalar.copy(
+            copy(
                 out=grouped[:].rearrange("p (c m i) -> p c i m", m=4, i=PACK),
-                in_=source[:].rearrange("p i (c m) -> p c i m", m=4),
+                in_=source.rearrange("p i (c m) -> p c i m", m=4),
             )
             return grouped
 
@@ -100,62 +120,59 @@ def tile_list_glu_resP_kernel(
             nc.vector.quantize_mx(out=codes[:].bitcast(FP8X4), scales=plane[:], in_=grouped[:])
             return codes, plane
 
-        def product(bank, codes, plane, c0, w_codes, w_plane):
-            nc.tensor.matmul_mx(
-                out=bank[:],
-                lhsT=codes[:, c0 : c0 + BLK].bitcast(FP8X4),
-                lhsT_scale=plane[:, c0 : c0 + BLK],
-                rhs=w_codes[:].bitcast(FP8X4),
-                rhs_scale=w_plane[:],
-                start=True,
-                stop=True,
-            )
+        def products(pool, name, codes, plane, w_codes, first):
+            width = codes.shape[1]
+            per_bank = BANK // width
+            banks = []
+            for i0 in range(0, PACK, per_bank):
+                bank = pool.tile([P, per_bank, width], F32, name=name)
+                for i in range(i0, i0 + per_bank):
+                    cols = slice(i * P, (i + 1) * P)
+                    nc.tensor.matmul_mx(
+                        out=bank[:, i - i0, :],
+                        lhsT=w_codes[:, cols].bitcast(FP8X4),
+                        lhsT_scale=w_planes[first:P, cols],
+                        rhs=codes[:].bitcast(FP8X4),
+                        rhs_scale=plane[:],
+                        start=True,
+                        stop=True,
+                    )
+                banks.append((bank, slice(i0, i0 + per_bank)))
+            return banks
 
-        x_picked = [keep.tile([P, PACK, X_CHUNK], F32, name=f"x_picked{c}") for c in range(J // X_CHUNK)]
-        for i in range(2):
-            for c in range(J // X_CHUNK):
-                gather(x_picked[c], x_planes, x_list, x_wgt[c][:], i, c * X_CHUNK, X_CHUNK)
-        gates = []
-        for c in range(J // X_CHUNK):
-            for i in range(2, PACK):
-                gather(x_picked[c], x_planes, x_list, x_wgt[c][:], i, c * X_CHUNK, X_CHUNK)
-            codes, plane = quantize(round_and_interleave(x_picked[c], f"x_bf{c}"), f"xq{c}")
-            for c0 in range(0, X_CHUNK, BLK):
-                bank = ps_a.tile([P, N], F32, name="ya")
-                product(bank, codes, plane, c0, wa_codes, wa_plane)
-                gate = keep.tile([P, PACK, P], F32, name=f"gate{len(gates)}")
-                nc.scalar.activation(out=gate[:], in_=bank[:].rearrange("j (q i) -> j i q", i=PACK), func=SILU)
-                gates.append(gate)
+        x_picked = keep.tile([P, PACK, J], F32, name="x_picked")
+        gather(x_picked, x_planes, x_list, x_wgt, 0, 0, HALF)
+        gather(x_picked, x_planes, x_list, x_wgt, 0, HALF, HALF)
+        for i in range(1, PACK - 1):
+            gather(x_picked, x_planes, x_list, x_wgt, i, 0, J)
+        gate = keep.tile([P, PACK, J], F32, name="gate")
+        for j0, w in spans(X_CHUNKS):
+            gather(x_picked, x_planes, x_list, x_wgt, PACK - 1, j0, w)
+            grouped = round_and_interleave(x_picked[:, :, j0 : j0 + w], f"x_bf{j0}", nc.scalar.copy)
+            codes, plane = quantize(grouped, f"xq{j0}")
+            for bank, rows in products(ps_a, "ya", codes, plane, wa_codes, WA_ROW):
+                nc.scalar.activation(out=gate[:, rows, j0 : j0 + w], in_=bank[:], func=SILU)
 
-        z_picked = [keep.tile([P, PACK, Z_CHUNK], F32, name=f"z_picked{c}") for c in range(J // Z_CHUNK)]
-        for i in range(PACK - 1):
-            for c in range(J // Z_CHUNK):
-                j0 = c * Z_CHUNK
-                gather(z_picked[c], z_planes, z_list, z_wgt[:, j0 : j0 + Z_CHUNK], i, j0, Z_CHUNK)
+        z_picked = keep.tile([P, PACK, J], F32, name="z_picked")
+        gather(z_picked, z_planes, z_list, z_wgt, 0, 0, HALF)
+        gather(z_picked, z_planes, z_list, z_wgt, 0, HALF, HALF)
+        for i in range(1, PACK - 1):
+            gather(z_picked, z_planes, z_list, z_wgt, i, 0, J)
         out_plane = keep.tile([P, J], U8, name="out_plane", align_bytes=64)
-        for c in range(J // Z_CHUNK):
-            j0 = c * Z_CHUNK
-            gather(z_picked[c], z_planes, z_list, z_wgt[:, j0 : j0 + Z_CHUNK], PACK - 1, j0, Z_CHUNK)
-            codes, plane = quantize(round_and_interleave(z_picked[c], f"z_bf{c}"), f"zq{c}")
-            result = keep.tile([P, PACK, OUT_CHUNK], F32, name=f"result{c}")
-            for c0 in range(0, Z_CHUNK, BLK):
-                bank = ps_b.tile([P, N], F32, name="yb")
-                product(bank, codes, plane, c0, wb_codes, wb_plane)
-                gated = ring.tile([P, PACK, P], F32, name="gated")
-                nc.vector.tensor_tensor(
-                    gated[:], bank[:].rearrange("j (q i) -> j i q", i=PACK), gates[(j0 + c0) // BLK][:], MULT
-                )
-                turned = ps_o.tile([P, PACK, BLK], F32, name="turned")
-                for i in range(PACK):
-                    nc.tensor.transpose(turned[:, i, :], gated[:, i, :], ident[:])
-                nc.vector.tensor_tensor(result[:, :, c0 : c0 + BLK], turned[:], res_t[c][:, :, c0 : c0 + BLK], ADD)
-            nc.sync.dma_start(out=out_rows[:, :, j0 : j0 + OUT_CHUNK], in_=result[:])
-            grouped = round_and_interleave(result, f"o_bf{c}")
-            o_codes = keep.tile([P, OUT_CHUNK], U32, name=f"o_codes{c}", align_bytes=64)
-            nc.vector.quantize_mx(
-                out=o_codes[:].bitcast(FP8X4), scales=out_plane[:, j0 : j0 + OUT_CHUNK], in_=grouped[:]
-            )
-            nc.sync.dma_start(out=out_words[:, j0 : j0 + OUT_CHUNK], in_=o_codes[:].bitcast(I32))
+        for c, (j0, w) in enumerate(spans(Z_CHUNKS)):
+            gather(z_picked, z_planes, z_list, z_wgt, PACK - 1, j0, w)
+            grouped = round_and_interleave(z_picked[:, :, j0 : j0 + w], f"z_bf{c}", nc.scalar.copy)
+            codes, plane = quantize(grouped, f"zq{c}")
+            result = keep.tile([P, PACK, w], F32, name=f"result{c}")
+            for bank, rows in products(ps_b, "yb", codes, plane, wb_codes, WB_ROW):
+                nc.vector.tensor_tensor(result[:, rows, :], bank[:], gate[:, rows, j0 : j0 + w], MULT)
+            nc.vector.tensor_tensor(result[:], result[:], res_t[c][:], ADD)
+            nc.sync.dma_start(out=out_rows[:, :, j0 : j0 + w], in_=result[:])
+            last = c == len(Z_CHUNKS) - 1
+            grouped = round_and_interleave(result[:], f"o_bf{c}", nc.vector.tensor_copy if last else nc.scalar.copy)
+            o_codes = keep.tile([P, w], U32, name=f"o_codes{c}", align_bytes=64)
+            nc.vector.quantize_mx(out=o_codes[:].bitcast(FP8X4), scales=out_plane[:, j0 : j0 + w], in_=grouped[:])
+            nc.sync.dma_start(out=out_words[:, j0 : j0 + w], in_=o_codes[:].bitcast(I32))
         for q in range(4):
             queue = nc.sync if q % 2 == 0 else nc.scalar
             queue.dma_start(

@@ -1,6 +1,7 @@
 from contextlib import ExitStack
 
 import concourse.mybir as mybir
+from concourse.masks import make_identity
 
 K, N, T, J = 512, 512, 2048, 1024
 FLOPS = 2 * 2 * K * N * J
@@ -23,6 +24,8 @@ WA_ROW, WB_ROW = 0, 4
 X_CHUNKS = (256, 256, 256, 256)
 Z_CHUNKS = (256, 256, 256, 128, 128)
 HALF = J // 2
+FIRST = 256
+TURNED = range(256, 512)
 
 
 def spans(widths):
@@ -35,8 +38,9 @@ def tile_list_glu_resP_kernel(
     nc = tc.nc
     with ExitStack() as ctx:
         keep = ctx.enter_context(tc.tile_pool(name="keep", bufs=1))
-        ps_a = ctx.enter_context(tc.psum_pool(name="ps_a", bufs=4))
-        ps_b = ctx.enter_context(tc.psum_pool(name="ps_b", bufs=4))
+        ring = ctx.enter_context(tc.tile_pool(name="ring", bufs=2))
+        ps_sum = ctx.enter_context(tc.psum_pool(name="ps_sum", bufs=6))
+        ps_total = ctx.enter_context(tc.psum_pool(name="ps_total", bufs=2))
 
         x_list = keep.tile([P, J // 16], U16, name="x_list")
         z_list = keep.tile([P, J // 16], U16, name="z_list")
@@ -46,9 +50,10 @@ def tile_list_glu_resP_kernel(
         z_wgt = keep.tile([P, J], F32, name="z_wgt")
         wa_codes = keep.tile([P, N], U32, name="wa_codes", align_bytes=64)
         wb_codes = keep.tile([P, N], U32, name="wb_codes", align_bytes=64)
-        wa_raw = keep.tile([P, N], U32, name="wa_raw")
-        wb_raw = keep.tile([P, N], U32, name="wb_raw")
-        w_planes_raw = keep.tile([P, N], U8, name="w_planes_raw")
+        wa_raw = keep.tile([P, N], U32, name="wa_raw", align_bytes=64)
+        wb_raw = keep.tile([P, N], U32, name="wb_raw", align_bytes=64)
+        w_planes_raw = keep.tile([P, N], U8, name="w_planes_raw", align_bytes=64)
+        ident = keep.tile([P, P], F32, name="ident")
         w_planes = keep.tile([P, N], U8, name="w_planes", align_bytes=64)
         res_t = [keep.tile([P, PACK, w], F32, name=f"res{j0}") for j0, w in spans(Z_CHUNKS)]
 
@@ -58,7 +63,8 @@ def tile_list_glu_resP_kernel(
         out_rows = out_0.rearrange("(p i) j -> p i j", i=PACK)
         out_words = out_1[0].rearrange("p j i -> p (j i)").bitcast(I32)
 
-        nc.vector.memset(w_planes_raw[:].bitcast(U32), 0)
+        nc.gpsimd.memset(w_planes_raw[:].bitcast(U32), 0)
+        make_identity(nc, ident[:])
 
         def load_scale_rows(first, scales, q):
             nc.sync.dma_start(
@@ -69,35 +75,47 @@ def tile_list_glu_resP_kernel(
         def load_words(codes, words):
             nc.sync.dma_start(out=codes[:].bitcast(I32), in_=words[0].rearrange("p n i -> p (n i)").bitcast(I32))
 
-        nc.sync.dma_start(out=x_planes[0][:], in_=x_rows[:, 0, :])
-        nc.sync.dma_start(x_list[:], offs)
-        nc.sync.dma_start(out=x_wgt[:, :HALF], in_=wgt[:, :HALF])
-        nc.sync.dma_start(out=x_wgt[:, HALF:], in_=wgt[:, HALF:])
-        for i in range(1, PACK - 1):
-            nc.sync.dma_start(out=x_planes[i][:], in_=x_rows[:, i, :])
-        load_words(wa_raw, wa_words)
-        nc.sync.dma_start(out=x_planes[PACK - 1][:], in_=x_rows[:, PACK - 1, :])
-        for q in range(4):
-            load_scale_rows(WA_ROW, wa_scales, q)
-        nc.sync.dma_start(z_list[:], offs2)
-        nc.sync.dma_start(out=z_wgt[:, :HALF], in_=wgt2[:, :HALF])
-        nc.sync.dma_start(out=z_planes[0][:], in_=z_rows[:, 0, :])
-        for q in range(4):
-            load_scale_rows(WB_ROW, wb_scales, q)
-        nc.sync.dma_start(out=z_wgt[:, HALF:], in_=wgt2[:, HALF:])
-        nc.sync.dma_start(out=z_planes[1][:], in_=z_rows[:, 1, :])
-        load_words(wb_raw, wb_words)
-        for i in range(2, PACK):
-            nc.sync.dma_start(out=z_planes[i][:], in_=z_rows[:, i, :])
-        for c, (j0, w) in enumerate(spans(Z_CHUNKS)):
+        def load_res(c):
+            j0, w = spans(Z_CHUNKS)[c]
             nc.sync.dma_start(out=res_t[c][:], in_=res_rows[:, :, j0 : j0 + w])
 
-        def deal_columns(dealt, raw, copy):
-            copy(out=dealt[:].rearrange("p (i m) -> p i m", i=PACK), in_=raw[:].rearrange("p (m i) -> p i m", i=PACK))
+        def load_plane(planes, rows, i):
+            nc.sync.dma_start(out=planes[i][:], in_=rows[:, i, :])
 
-        deal_columns(wa_codes, wa_raw, nc.scalar.copy)
-        deal_columns(w_planes, w_planes_raw, nc.vector.tensor_copy)
-        deal_columns(wb_codes, wb_raw, nc.scalar.copy)
+        load_plane(x_planes, x_rows, 0)
+        nc.sync.dma_start(x_list[:], offs)
+        nc.sync.dma_start(out=x_wgt[:, :FIRST], in_=wgt[:, :FIRST])
+        nc.sync.dma_start(out=x_wgt[:, FIRST:], in_=wgt[:, FIRST:])
+        scale_rows = [(first, scales, q) for first, scales in ((WA_ROW, wa_scales), (WB_ROW, wb_scales)) for q in range(4)]
+        for i in range(1, PACK):
+            if i == PACK - 1:
+                load_words(wa_raw, wa_words)
+            load_plane(x_planes, x_rows, i)
+            for rows in scale_rows[3 * (i - 1) : 3 * i]:
+                load_scale_rows(*rows)
+        nc.sync.dma_start(z_list[:], offs2)
+        nc.sync.dma_start(out=z_wgt[:], in_=wgt2)
+        load_plane(z_planes, z_rows, 0)
+        load_words(wb_raw, wb_words)
+        load_plane(z_planes, z_rows, 1)
+        turned_chunks = [c for c, (j0, w) in enumerate(spans(Z_CHUNKS)) if j0 in TURNED]
+        for c in turned_chunks:
+            load_res(c)
+        load_plane(z_planes, z_rows, 2)
+        load_plane(z_planes, z_rows, 3)
+        for c in range(len(Z_CHUNKS)):
+            if c not in turned_chunks:
+                load_res(c)
+
+        def deal_columns(dealt, raw, run, copy):
+            copy(
+                out=dealt[:].rearrange("p (i c m) -> p c i m", i=PACK, m=run),
+                in_=raw[:].rearrange("p (c m i) -> p c i m", i=PACK, m=run),
+            )
+
+        deal_columns(wa_codes, wa_raw, 4, nc.scalar.copy)
+        deal_columns(w_planes, w_planes_raw, 16, nc.vector.tensor_copy)
+        deal_columns(wb_codes, wb_raw, 4, nc.scalar.copy)
 
         def gather(picked, planes, offsets, weights, i, j0, width):
             cols = offsets[:, j0 // 16 : (j0 + width) // 16]
@@ -140,33 +158,84 @@ def tile_list_glu_resP_kernel(
                 banks.append((bank, slice(i0, i0 + per_bank)))
             return banks
 
+        def turned_product(pool, name, codes, plane, c0, w_raw, first):
+            bank = pool.tile([P, N], F32, name=name)
+            nc.tensor.matmul_mx(
+                out=bank[:],
+                lhsT=codes[:, c0 : c0 + P].bitcast(FP8X4),
+                lhsT_scale=plane[:, c0 : c0 + P],
+                rhs=w_raw[:].bitcast(FP8X4),
+                rhs_scale=w_planes_raw[first:P, :],
+                start=True,
+                stop=True,
+            )
+            return bank[:].rearrange("j (m i) -> j i m", i=PACK)
+
+        def add_turned(total, part, start, stop):
+            for i in range(PACK):
+                nc.tensor.matmul(
+                    total[:, i, :],
+                    part[:, i, :],
+                    ident[:],
+                    start=start and i == 0,
+                    stop=stop and i == PACK - 1,
+                    is_transpose=True,
+                )
+
         x_picked = keep.tile([P, PACK, J], F32, name="x_picked")
-        gather(x_picked, x_planes, x_list, x_wgt, 0, 0, HALF)
-        gather(x_picked, x_planes, x_list, x_wgt, 0, HALF, HALF)
+        gather(x_picked, x_planes, x_list, x_wgt, 0, 0, FIRST)
+        gather(x_picked, x_planes, x_list, x_wgt, 0, FIRST, J - FIRST)
         for i in range(1, PACK - 1):
             gather(x_picked, x_planes, x_list, x_wgt, i, 0, J)
-        gate = keep.tile([P, PACK, J], F32, name="gate")
+        x_grouped = []
         for j0, w in spans(X_CHUNKS):
             gather(x_picked, x_planes, x_list, x_wgt, PACK - 1, j0, w)
-            grouped = round_and_interleave(x_picked[:, :, j0 : j0 + w], f"x_bf{j0}", nc.scalar.copy)
-            codes, plane = quantize(grouped, f"xq{j0}")
-            for bank, rows in products(ps_a, "ya", codes, plane, wa_codes, WA_ROW):
-                nc.scalar.activation(out=gate[:, rows, j0 : j0 + w], in_=bank[:], func=SILU)
+            x_grouped.append(round_and_interleave(x_picked[:, :, j0 : j0 + w], f"x_bf{j0}", nc.scalar.copy))
+        gate = keep.tile([P, PACK, J], F32, name="gate")
+        for c, (j0, w) in enumerate(spans(X_CHUNKS)):
+            codes, plane = quantize(x_grouped[c], f"xq{j0}")
+            if j0 in TURNED:
+                for c0 in range(0, w, P):
+                    sums = turned_product(ps_sum, "sums", codes, plane, c0, wa_raw, WA_ROW)
+                    nc.scalar.activation(out=gate[:, :, j0 + c0 : j0 + c0 + P], in_=sums, func=SILU)
+            else:
+                for bank, rows in products(ps_sum, "sums", codes, plane, wa_codes, WA_ROW):
+                    nc.scalar.activation(out=gate[:, rows, j0 : j0 + w], in_=bank[:], func=SILU)
+
+        totals = {}
+        for c in turned_chunks:
+            j0, w = spans(Z_CHUNKS)[c]
+            for c0 in range(0, w, P):
+                bank = ps_sum.tile([P, PACK, P], F32, name="sums")
+                for i in range(PACK):
+                    nc.tensor.transpose(bank[:, i, :], res_t[c][:, i, c0 : c0 + P], ident[:])
+                turned_res = ring.tile([P, PACK, P], F32, name="turned_res")
+                nc.scalar.copy(out=turned_res[:], in_=bank[:])
+                totals[j0 + c0] = ps_total.tile([P, PACK, P], F32, name="total")
+                add_turned(totals[j0 + c0], turned_res, True, False)
 
         z_picked = keep.tile([P, PACK, J], F32, name="z_picked")
-        gather(z_picked, z_planes, z_list, z_wgt, 0, 0, HALF)
-        gather(z_picked, z_planes, z_list, z_wgt, 0, HALF, HALF)
-        for i in range(1, PACK - 1):
+        for i in range(PACK - 1):
             gather(z_picked, z_planes, z_list, z_wgt, i, 0, J)
-        out_plane = keep.tile([P, J], U8, name="out_plane", align_bytes=64)
+        z_grouped = []
         for c, (j0, w) in enumerate(spans(Z_CHUNKS)):
             gather(z_picked, z_planes, z_list, z_wgt, PACK - 1, j0, w)
-            grouped = round_and_interleave(z_picked[:, :, j0 : j0 + w], f"z_bf{c}", nc.scalar.copy)
-            codes, plane = quantize(grouped, f"zq{c}")
+            z_grouped.append(round_and_interleave(z_picked[:, :, j0 : j0 + w], f"z_bf{c}", nc.scalar.copy))
+        out_plane = keep.tile([P, J], U8, name="out_plane", align_bytes=64)
+        for c, (j0, w) in enumerate(spans(Z_CHUNKS)):
+            codes, plane = quantize(z_grouped[c], f"zq{c}")
             result = keep.tile([P, PACK, w], F32, name=f"result{c}")
-            for bank, rows in products(ps_b, "yb", codes, plane, wb_codes, WB_ROW):
-                nc.vector.tensor_tensor(result[:, rows, :], bank[:], gate[:, rows, j0 : j0 + w], MULT)
-            nc.vector.tensor_tensor(result[:], result[:], res_t[c][:], ADD)
+            if j0 in TURNED:
+                for c0 in range(0, w, P):
+                    sums = turned_product(ps_sum, "sums", codes, plane, c0, wb_raw, WB_ROW)
+                    gated = ring.tile([P, PACK, P], F32, name="gated")
+                    nc.vector.tensor_tensor(gated[:], sums, gate[:, :, j0 + c0 : j0 + c0 + P], MULT)
+                    add_turned(totals[j0 + c0], gated, False, True)
+                    nc.scalar.copy(out=result[:, :, c0 : c0 + P], in_=totals[j0 + c0][:])
+            else:
+                for bank, rows in products(ps_sum, "sums", codes, plane, wb_codes, WB_ROW):
+                    nc.vector.tensor_tensor(result[:, rows, :], bank[:], gate[:, rows, j0 : j0 + w], MULT)
+                nc.vector.tensor_tensor(result[:], result[:], res_t[c][:], ADD)
             nc.sync.dma_start(out=out_rows[:, :, j0 : j0 + w], in_=result[:])
             last = c == len(Z_CHUNKS) - 1
             grouped = round_and_interleave(result[:], f"o_bf{c}", nc.vector.tensor_copy if last else nc.scalar.copy)

@@ -25,6 +25,14 @@ X_CHUNKS = (256, 256, 256, 256)
 Z_CHUNKS = (256, 256, 256, 128, 128)
 HALF = J // 2
 FIRST = 256
+SPARE = 384
+PS = 6
+R1 = 9
+GB = 2
+HOLDER = 0
+FIRST_HELD = 4
+AHEAD = 2
+V_ROUNDS = 1
 TURNED = range(256, 512)
 
 
@@ -38,9 +46,9 @@ def tile_list_glu_resP_kernel(
     nc = tc.nc
     with ExitStack() as ctx:
         keep = ctx.enter_context(tc.tile_pool(name="keep", bufs=1))
-        ring = ctx.enter_context(tc.tile_pool(name="ring", bufs=2))
-        ps_sum = ctx.enter_context(tc.psum_pool(name="ps_sum", bufs=6))
-        ps_total = ctx.enter_context(tc.psum_pool(name="ps_total", bufs=2))
+        ring = ctx.enter_context(tc.tile_pool(name="ring", bufs=GB))
+        ps_sum = ctx.enter_context(tc.psum_pool(name="ps_sum", bufs=PS))
+        ps_total = ctx.enter_context(tc.psum_pool(name="ps_total", bufs=8 - PS))
 
         x_list = keep.tile([P, J // 16], U16, name="x_list")
         z_list = keep.tile([P, J // 16], U16, name="z_list")
@@ -99,9 +107,11 @@ def tile_list_glu_resP_kernel(
         load_words(wb_raw, wb_words)
         load_plane(z_planes, z_rows, 1)
         turned_chunks = [c for c, (j0, w) in enumerate(spans(Z_CHUNKS)) if j0 in TURNED]
-        for c in turned_chunks:
+        for c in turned_chunks[:R1]:
             load_res(c)
         load_plane(z_planes, z_rows, 2)
+        for c in turned_chunks[R1:]:
+            load_res(c)
         load_plane(z_planes, z_rows, 3)
         for c in range(len(Z_CHUNKS)):
             if c not in turned_chunks:
@@ -214,30 +224,64 @@ def tile_list_glu_resP_kernel(
                 totals[j0 + c0] = ps_total.tile([P, PACK, P], F32, name="total")
                 add_turned(totals[j0 + c0], turned_res, True, False)
 
-        z_picked = keep.tile([P, PACK, J], F32, name="z_picked")
+        z_flat = keep.tile([P, PACK * J + SPARE], F32, name="z_picked", align_bytes=64)
+        z_picked = z_flat[:, : PACK * J].rearrange("p (i j) -> p i j", i=PACK)
         for i in range(PACK - 1):
             gather(z_picked, z_planes, z_list, z_wgt, i, 0, J)
-        z_grouped = []
-        for c, (j0, w) in enumerate(spans(Z_CHUNKS)):
+        z_grouped, z_sums = {}, {}
+
+        def pick_last(c):
+            j0, w = spans(Z_CHUNKS)[c]
             gather(z_picked, z_planes, z_list, z_wgt, PACK - 1, j0, w)
-            z_grouped.append(round_and_interleave(z_picked[:, :, j0 : j0 + w], f"z_bf{c}", nc.scalar.copy))
-        out_plane = keep.tile([P, J], U8, name="out_plane", align_bytes=64)
-        for c, (j0, w) in enumerate(spans(Z_CHUNKS)):
+
+        def group(c):
+            j0, w = spans(Z_CHUNKS)[c]
+            if c == HOLDER:
+                at = (PACK - 1) * J + spans(Z_CHUNKS)[FIRST_HELD][0]
+                grouped = z_flat[:, at : at + w * PACK // 2].bitcast(BF16)
+                nc.scalar.copy(
+                    out=grouped.rearrange("p (c m i) -> p c i m", m=4, i=PACK),
+                    in_=z_picked[:, :, j0 : j0 + w].rearrange("p i (c m) -> p c i m", m=4),
+                )
+                z_grouped[c] = grouped
+            else:
+                z_grouped[c] = round_and_interleave(z_picked[:, :, j0 : j0 + w], f"z_bf{c}", nc.scalar.copy)
+
+        def multiply(c):
+            j0, w = spans(Z_CHUNKS)[c]
             codes, plane = quantize(z_grouped[c], f"zq{c}")
+            if j0 in TURNED:
+                z_sums[c] = [turned_product(ps_sum, "sums", codes, plane, c0, wb_raw, WB_ROW) for c0 in range(0, w, P)]
+            else:
+                z_sums[c] = products(ps_sum, "sums", codes, plane, wb_codes, WB_ROW)
+            if c == HOLDER:
+                for h in range(FIRST_HELD, len(Z_CHUNKS)):
+                    pick_last(h)
+                    group(h)
+
+        for c in range(FIRST_HELD):
+            pick_last(c)
+        for c in range(FIRST_HELD):
+            group(c)
+        out_plane = keep.tile([P, J], U8, name="out_plane", align_bytes=64)
+        for c in range(AHEAD):
+            multiply(c)
+        for c, (j0, w) in enumerate(spans(Z_CHUNKS)):
+            if c + AHEAD < len(Z_CHUNKS):
+                multiply(c + AHEAD)
             result = keep.tile([P, PACK, w], F32, name=f"result{c}")
             if j0 in TURNED:
-                for c0 in range(0, w, P):
-                    sums = turned_product(ps_sum, "sums", codes, plane, c0, wb_raw, WB_ROW)
+                for k, c0 in enumerate(range(0, w, P)):
                     gated = ring.tile([P, PACK, P], F32, name="gated")
-                    nc.vector.tensor_tensor(gated[:], sums, gate[:, :, j0 + c0 : j0 + c0 + P], MULT)
+                    nc.vector.tensor_tensor(gated[:], z_sums[c][k], gate[:, :, j0 + c0 : j0 + c0 + P], MULT)
                     add_turned(totals[j0 + c0], gated, False, True)
                     nc.scalar.copy(out=result[:, :, c0 : c0 + P], in_=totals[j0 + c0][:])
             else:
-                for bank, rows in products(ps_sum, "sums", codes, plane, wb_codes, WB_ROW):
+                for bank, rows in z_sums[c]:
                     nc.vector.tensor_tensor(result[:, rows, :], bank[:], gate[:, rows, j0 : j0 + w], MULT)
                 nc.vector.tensor_tensor(result[:], result[:], res_t[c][:], ADD)
             nc.sync.dma_start(out=out_rows[:, :, j0 : j0 + w], in_=result[:])
-            last = c == len(Z_CHUNKS) - 1
+            last = c >= len(Z_CHUNKS) - V_ROUNDS
             grouped = round_and_interleave(result[:], f"o_bf{c}", nc.vector.tensor_copy if last else nc.scalar.copy)
             o_codes = keep.tile([P, w], U32, name=f"o_codes{c}", align_bytes=64)
             nc.vector.quantize_mx(out=o_codes[:].bitcast(FP8X4), scales=out_plane[:, j0 : j0 + w], in_=grouped[:])

from contextlib import ExitStack

import concourse.mybir as mybir
from concourse.masks import make_identity

K, N, T, J = 512, 512, 2048, 1024
FLOPS = 2 * 2 * K * N * J

F32 = mybir.dt.float32
BF16 = mybir.dt.bfloat16
I32 = mybir.dt.int32
U32 = mybir.dt.uint32
U16 = mybir.dt.uint16
U8 = mybir.dt.uint8
FP8X4 = mybir.dt.float8_e4m3fn_x4
MULT = mybir.AluOpType.mult
ADD = mybir.AluOpType.add
SILU = mybir.ActivationFunctionType.Silu

P = 128
PACK = 4
BANK = 512
WA_ROW, WB_ROW = 0, 4
X_CHUNKS = (256, 256, 256, 256)
Z_CHUNKS = (256, 256, 256, 128, 128)
HALF = J // 2
FIRST = 256
SPARE = 384
PS = 6
R1 = 9
GB = 2
HOLDER = 0
FIRST_HELD = 4
AHEAD = 2
V_ROUNDS = 1
TURNED = range(256, 512)


def spans(widths):
    return [(sum(widths[:c]), w) for c, w in enumerate(widths)]


def tile_list_glu_resP_kernel(
    tc, xT, wgt, zT, wgt2, wa_words, wa_scales, wb_words, wb_scales, res, offs, offs2, out_0, out_1, out_2
):
    nc = tc.nc
    with ExitStack() as ctx:
        keep = ctx.enter_context(tc.tile_pool(name="keep", bufs=1))
        ring = ctx.enter_context(tc.tile_pool(name="ring", bufs=GB))
        ps_sum = ctx.enter_context(tc.psum_pool(name="ps_sum", bufs=PS))
        ps_total = ctx.enter_context(tc.psum_pool(name="ps_total", bufs=8 - PS))

        x_list = keep.tile([P, J // 16], U16, name="x_list")
        z_list = keep.tile([P, J // 16], U16, name="z_list")
        x_planes = [keep.tile([P, T], F32, name=f"x_plane{i}") for i in range(PACK)]
        z_planes = [keep.tile([P, T], F32, name=f"z_plane{i}") for i in range(PACK)]
        x_wgt = keep.tile([P, J], F32, name="x_wgt")
        z_wgt = keep.tile([P, J], F32, name="z_wgt")
        wa_codes = keep.tile([P, N], U32, name="wa_codes", align_bytes=64)
        wb_codes = keep.tile([P, N], U32, name="wb_codes", align_bytes=64)
        wa_raw = keep.tile([P, N], U32, name="wa_raw", align_bytes=64)
        wb_raw = keep.tile([P, N], U32, name="wb_raw", align_bytes=64)
        w_planes_raw = keep.tile([P, N], U8, name="w_planes_raw", align_bytes=64)
        ident = keep.tile([P, P], F32, name="ident")
        w_planes = keep.tile([P, N], U8, name="w_planes", align_bytes=64)
        res_t = [keep.tile([P, PACK, w], F32, name=f"res{j0}") for j0, w in spans(Z_CHUNKS)]

        x_rows = xT.rearrange("(p i) t -> p i t", i=PACK)
        z_rows = zT.rearrange("(p i) t -> p i t", i=PACK)
        res_rows = res.rearrange("(p i) j -> p i j", i=PACK)
        out_rows = out_0.rearrange("(p i) j -> p i j", i=PACK)
        out_words = out_1[0].rearrange("p j i -> p (j i)").bitcast(I32)

        nc.gpsimd.memset(w_planes_raw[:].bitcast(U32), 0)
        make_identity(nc, ident[:])

        def load_scale_rows(first, scales, q):
            nc.sync.dma_start(
                out=w_planes_raw[32 * q + first : 32 * q + first + 4, :].bitcast(I32),
                in_=scales[0, 4 * q : 4 * q + 4, :].bitcast(I32),
            )

        def load_words(codes, words):
            nc.sync.dma_start(out=codes[:].bitcast(I32), in_=words[0].rearrange("p n i -> p (n i)").bitcast(I32))

        def load_res(c):
            j0, w = spans(Z_CHUNKS)[c]
            nc.sync.dma_start(out=res_t[c][:], in_=res_rows[:, :, j0 : j0 + w])

        def load_plane(planes, rows, i):
            nc.sync.dma_start(out=planes[i][:], in_=rows[:, i, :])

        load_plane(x_planes, x_rows, 0)
        nc.sync.dma_start(x_list[:], offs)
        nc.sync.dma_start(out=x_wgt[:, :FIRST], in_=wgt[:, :FIRST])
        nc.sync.dma_start(out=x_wgt[:, FIRST:], in_=wgt[:, FIRST:])
        scale_rows = [(first, scales, q) for first, scales in ((WA_ROW, wa_scales), (WB_ROW, wb_scales)) for q in range(4)]
        for i in range(1, PACK):
            if i == PACK - 1:
                load_words(wa_raw, wa_words)
            load_plane(x_planes, x_rows, i)
            for rows in scale_rows[3 * (i - 1) : 3 * i]:
                load_scale_rows(*rows)
        nc.sync.dma_start(z_list[:], offs2)
        nc.sync.dma_start(out=z_wgt[:], in_=wgt2)
        load_plane(z_planes, z_rows, 0)
        load_words(wb_raw, wb_words)
        load_plane(z_planes, z_rows, 1)
        turned_chunks = [c for c, (j0, w) in enumerate(spans(Z_CHUNKS)) if j0 in TURNED]
        for c in turned_chunks[:R1]:
            load_res(c)
        load_plane(z_planes, z_rows, 2)
        for c in turned_chunks[R1:]:
            load_res(c)
        load_plane(z_planes, z_rows, 3)
        for c in range(len(Z_CHUNKS)):
            if c not in turned_chunks:
                load_res(c)

        def deal_columns(dealt, raw, run, copy):
            copy(
                out=dealt[:].rearrange("p (i c m) -> p c i m", i=PACK, m=run),
                in_=raw[:].rearrange("p (c m i) -> p c i m", i=PACK, m=run),
            )

        deal_columns(wa_codes, wa_raw, 4, nc.scalar.copy)
        deal_columns(w_planes, w_planes_raw, 16, nc.vector.tensor_copy)
        deal_columns(wb_codes, wb_raw, 4, nc.scalar.copy)

        def gather(picked, planes, offsets, weights, i, j0, width):
            cols = offsets[:, j0 // 16 : (j0 + width) // 16]
            span = slice(j0, j0 + width)
            nc.vector.tensor_tensor(picked[:, i, span], planes[i][:].indirect(cols), weights[:, span], MULT)

        def round_and_interleave(source, name, copy):
            width = source.shape[2]
            grouped = keep.tile([P, width * PACK], BF16, name=name, align_bytes=64)
            copy(
                out=grouped[:].rearrange("p (c m i) -> p c i m", m=4, i=PACK),
                in_=source.rearrange("p i (c m) -> p c i m", m=4),
            )
            return grouped

        def quantize(grouped, name):
            width = grouped.shape[1] // PACK
            codes = keep.tile([P, width], U32, name=name + "_codes", align_bytes=64)
            plane = keep.tile([P, width], U8, name=name + "_plane", align_bytes=64)
            nc.vector.quantize_mx(out=codes[:].bitcast(FP8X4), scales=plane[:], in_=grouped[:])
            return codes, plane

        def products(pool, name, codes, plane, w_codes, first):
            width = codes.shape[1]
            per_bank = BANK // width
            banks = []
            for i0 in range(0, PACK, per_bank):
                bank = pool.tile([P, per_bank, width], F32, name=name)
                for i in range(i0, i0 + per_bank):
                    cols = slice(i * P, (i + 1) * P)
                    nc.tensor.matmul_mx(
                        out=bank[:, i - i0, :],
                        lhsT=w_codes[:, cols].bitcast(FP8X4),
                        lhsT_scale=w_planes[first:P, cols],
                        rhs=codes[:].bitcast(FP8X4),
                        rhs_scale=plane[:],
                        start=True,
                        stop=True,
                    )
                banks.append((bank, slice(i0, i0 + per_bank)))
            return banks

        def turned_product(pool, name, codes, plane, c0, w_raw, first):
            bank = pool.tile([P, N], F32, name=name)
            nc.tensor.matmul_mx(
                out=bank[:],
                lhsT=codes[:, c0 : c0 + P].bitcast(FP8X4),
                lhsT_scale=plane[:, c0 : c0 + P],
                rhs=w_raw[:].bitcast(FP8X4),
                rhs_scale=w_planes_raw[first:P, :],
                start=True,
                stop=True,
            )
            return bank[:].rearrange("j (m i) -> j i m", i=PACK)

        def add_turned(total, part, start, stop):
            for i in range(PACK):
                nc.tensor.matmul(
                    total[:, i, :],
                    part[:, i, :],
                    ident[:],
                    start=start and i == 0,
                    stop=stop and i == PACK - 1,
                    is_transpose=True,
                )

        x_picked = keep.tile([P, PACK, J], F32, name="x_picked")
        gather(x_picked, x_planes, x_list, x_wgt, 0, 0, FIRST)
        gather(x_picked, x_planes, x_list, x_wgt, 0, FIRST, J - FIRST)
        for i in range(1, PACK - 1):
            gather(x_picked, x_planes, x_list, x_wgt, i, 0, J)
        x_grouped = []
        for j0, w in spans(X_CHUNKS):
            gather(x_picked, x_planes, x_list, x_wgt, PACK - 1, j0, w)
            x_grouped.append(round_and_interleave(x_picked[:, :, j0 : j0 + w], f"x_bf{j0}", nc.scalar.copy))
        gate = keep.tile([P, PACK, J], F32, name="gate")
        for c, (j0, w) in enumerate(spans(X_CHUNKS)):
            codes, plane = quantize(x_grouped[c], f"xq{j0}")
            if j0 in TURNED:
                for c0 in range(0, w, P):
                    sums = turned_product(ps_sum, "sums", codes, plane, c0, wa_raw, WA_ROW)
                    nc.scalar.activation(out=gate[:, :, j0 + c0 : j0 + c0 + P], in_=sums, func=SILU)
            else:
                for bank, rows in products(ps_sum, "sums", codes, plane, wa_codes, WA_ROW):
                    nc.scalar.activation(out=gate[:, rows, j0 : j0 + w], in_=bank[:], func=SILU)

        totals = {}
        for c in turned_chunks:
            j0, w = spans(Z_CHUNKS)[c]
            for c0 in range(0, w, P):
                bank = ps_sum.tile([P, PACK, P], F32, name="sums")
                for i in range(PACK):
                    nc.tensor.transpose(bank[:, i, :], res_t[c][:, i, c0 : c0 + P], ident[:])
                turned_res = ring.tile([P, PACK, P], F32, name="turned_res")
                nc.scalar.copy(out=turned_res[:], in_=bank[:])
                totals[j0 + c0] = ps_total.tile([P, PACK, P], F32, name="total")
                add_turned(totals[j0 + c0], turned_res, True, False)

        z_flat = keep.tile([P, PACK * J + SPARE], F32, name="z_picked", align_bytes=64)
        z_picked = z_flat[:, : PACK * J].rearrange("p (i j) -> p i j", i=PACK)
        for i in range(PACK - 1):
            gather(z_picked, z_planes, z_list, z_wgt, i, 0, J)
        z_grouped, z_sums = {}, {}

        def pick_last(c):
            j0, w = spans(Z_CHUNKS)[c]
            gather(z_picked, z_planes, z_list, z_wgt, PACK - 1, j0, w)

        def group(c):
            j0, w = spans(Z_CHUNKS)[c]
            if c == HOLDER:
                at = (PACK - 1) * J + spans(Z_CHUNKS)[FIRST_HELD][0]
                grouped = z_flat[:, at : at + w * PACK // 2].bitcast(BF16)
                nc.scalar.copy(
                    out=grouped.rearrange("p (c m i) -> p c i m", m=4, i=PACK),
                    in_=z_picked[:, :, j0 : j0 + w].rearrange("p i (c m) -> p c i m", m=4),
                )
                z_grouped[c] = grouped
            else:
                z_grouped[c] = round_and_interleave(z_picked[:, :, j0 : j0 + w], f"z_bf{c}", nc.scalar.copy)

        def multiply(c):
            j0, w = spans(Z_CHUNKS)[c]
            codes, plane = quantize(z_grouped[c], f"zq{c}")
            if j0 in TURNED:
                z_sums[c] = [turned_product(ps_sum, "sums", codes, plane, c0, wb_raw, WB_ROW) for c0 in range(0, w, P)]
            else:
                z_sums[c] = products(ps_sum, "sums", codes, plane, wb_codes, WB_ROW)
            if c == HOLDER:
                for h in range(FIRST_HELD, len(Z_CHUNKS)):
                    pick_last(h)
                    group(h)

        for c in range(FIRST_HELD):
            pick_last(c)
        for c in range(FIRST_HELD):
            group(c)
        out_plane = keep.tile([P, J], U8, name="out_plane", align_bytes=64)
        for c in range(AHEAD):
            multiply(c)
        for c, (j0, w) in enumerate(spans(Z_CHUNKS)):
            if c + AHEAD < len(Z_CHUNKS):
                multiply(c + AHEAD)
            result = keep.tile([P, PACK, w], F32, name=f"result{c}")
            if j0 in TURNED:
                for k, c0 in enumerate(range(0, w, P)):
                    gated = ring.tile([P, PACK, P], F32, name="gated")
                    nc.vector.tensor_tensor(gated[:], z_sums[c][k], gate[:, :, j0 + c0 : j0 + c0 + P], MULT)
                    add_turned(totals[j0 + c0], gated, False, True)
                    nc.scalar.copy(out=result[:, :, c0 : c0 + P], in_=totals[j0 + c0][:])
            else:
                for bank, rows in z_sums[c]:
                    nc.vector.tensor_tensor(result[:, rows, :], bank[:], gate[:, rows, j0 : j0 + w], MULT)
                nc.vector.tensor_tensor(result[:], result[:], res_t[c][:], ADD)
            nc.sync.dma_start(out=out_rows[:, :, j0 : j0 + w], in_=result[:])
            last = c >= len(Z_CHUNKS) - V_ROUNDS
            grouped = round_and_interleave(result[:], f"o_bf{c}", nc.vector.tensor_copy if last else nc.scalar.copy)
            o_codes = keep.tile([P, w], U32, name=f"o_codes{c}", align_bytes=64)
            nc.vector.quantize_mx(out=o_codes[:].bitcast(FP8X4), scales=out_plane[:, j0 : j0 + w], in_=grouped[:])
            nc.sync.dma_start(out=out_words[:, j0 : j0 + w], in_=o_codes[:].bitcast(I32))
        for q in range(4):
            queue = nc.sync if q % 2 == 0 else nc.scalar
            queue.dma_start(
                out=out_2[0, 4 * q : 4 * q + 4, :].bitcast(I32),
                in_=out_plane[32 * q : 32 * q + 4, :].bitcast(I32),
            )
